import numpy as np
import ml_dtypes


def mxq(x, axis, fmt="e4m3"):
    dtype, down = {"e4m3": (ml_dtypes.float8_e4m3fn, 7), "e5m2": (ml_dtypes.float8_e5m2, 14)}[fmt]
    v = np.moveaxis(np.asarray(x, np.float32).astype(ml_dtypes.bfloat16).astype(np.float64), axis, -1)
    blocks = v.reshape(v.shape[:-1] + (-1, 32))
    amax = np.abs(blocks).max(-1, keepdims=True)
    byte = np.maximum(np.where(amax > 0, np.frexp(amax)[1] - 1 + 127, 0) - down, 1)
    scale = np.exp2(byte - 127.0)
    codes = (blocks / scale).astype(np.float32).astype(dtype).astype(np.float64)
    return np.moveaxis((codes * scale).reshape(v.shape), -1, axis)


WIDE = False


def mx_kscale(k):
    if not WIDE:
        return np.ones(k)
    levels = np.array([10, -10, 5, -5, 0])
    if k % 512:
        return np.exp2(np.random.permutation(np.resize(levels, k // 32))).repeat(32)
    a = np.empty((k // 512, 16))
    for p in range(k // 512):
        a[p, :8] = np.random.permutation(np.resize(levels, 8))
        for g in range(8):
            far = levels[np.abs(levels - a[p, g]) >= 10]
            a[p, g + 8] = far[np.random.randint(len(far))]
    return np.exp2(a.ravel()).repeat(32)


def f64(x):
    return np.asarray(x).astype(np.float64)


def striped8(idx):
    return np.concatenate([x.reshape(-1, 16).T for x in idx]).astype(np.uint16)


def runs(offs, k):
    lists = np.stack([offs[16 * r : 16 * r + 16].T.reshape(-1) for r in range(8)]).astype(np.int64)
    return lists[np.arange(k) % 512 // 64]


def pack_weight(w):
    k, n = w.shape
    w = f64(np.asarray(w, np.float32).astype(ml_dtypes.bfloat16)).reshape(k // 32, 32, n)
    amax = np.abs(w).max(1)
    byte = np.clip(np.where(amax > 0, np.frexp(amax)[1] - 1 + 127 - 7, 1), 1, 254)
    scaled = (w * np.exp2(127.0 - byte)[:, None, :]).reshape(k, n).astype(np.float32)
    words = np.ascontiguousarray(scaled.reshape(k // 512, 128, 4, n).transpose(0, 1, 3, 2)).astype(ml_dtypes.float8_e4m3fn).view(np.uint8)
    return words, np.ascontiguousarray(byte.astype(np.uint8).reshape(k // 512, 16, n))


def unpack_weight(words, scales):
    g, p, n, _ = words.shape
    vals = np.ascontiguousarray(words).view(ml_dtypes.float8_e4m3fn).astype(np.float64) * np.repeat(np.exp2(scales.astype(np.float64) - 127.0), 8, axis=1)[..., None]
    return vals.transpose(0, 1, 3, 2).reshape(g * 512, n)


def relu(v):
    return np.maximum(v, 0.0)


def sigmoid(v):
    return 1.0 / (1.0 + np.exp(-np.maximum(v, -700.0)))


K, T, S, N, H = 512, 2048, 512, 512, 512


def setup_inputs():
    n = np.random.standard_normal
    s = mx_kscale(K)[:, None]
    u = mx_kscale(H)
    packed_xT = pack_weight(n((K, T)) * s)
    return {
        "x_words": packed_xT[0],
        "x_scales": packed_xT[1],
        "w1": (n((K, H)) / np.sqrt(K) / s).astype(np.float32),
        "gn": (np.random.uniform(0.5, 1.5, (H, 1)) * u[:, None]).astype(np.float32),
        "w2": (n((H, N)) / np.sqrt(H) / u[:, None]).astype(np.float32),
        "offs": striped8(np.random.randint(0, T, (8, S))),
        "n1": striped8(np.stack([np.random.permutation(S) for _ in range(8)])),
        "n2": striped8(np.stack([np.random.permutation(S) for _ in range(8)])),
    }


def reference(x_words, x_scales, w1, gn, w2, offs, n1, n2):
    xq = unpack_weight(x_words, x_scales)[np.arange(K)[:, None], runs(offs, K)]
    y = mxq(f64(w1), 0, "e4m3").T @ xq
    a = y[np.arange(H)[:, None], runs(n1, H)]
    z = f64(gn) * (relu(y - a) * (sigmoid(y + y[np.arange(H)[:, None], runs(n2, H)])))
    return mxq(f64(w2), 0, "e4m3").T @ mxq(z, 0, "e4m3")

@@ -1,0 +1,173 @@
+from contextlib import ExitStack
+
+import concourse.mybir as mybir
+
+K, T, S, H, N = 512, 2048, 512, 512, 512
+FLOPS = 2 * K * H * S + 2 * H * N * S
+
+F32 = mybir.dt.float32
+BF16 = mybir.dt.bfloat16
+I32 = mybir.dt.int32
+U32 = mybir.dt.uint32
+U16 = mybir.dt.uint16
+U8 = mybir.dt.uint8
+FP8X4 = mybir.dt.float8_e4m3fn_x4
+ALU = mybir.AluOpType
+ACT = mybir.ActivationFunctionType
+
+P = 128
+PACK = 4
+HALF = 256
+CHUNKS = (256, 128, 128)
+
+
+def tile_picked_hashgate_none_p_kernel(tc, x_words, x_scales, w1, gn, w2, offs, n1, n2, out):
+    nc = tc.nc
+    with ExitStack() as ctx:
+        keep = ctx.enter_context(tc.tile_pool(name="keep", bufs=1))
+        ring = ctx.enter_context(tc.tile_pool(name="ring", bufs=3))
+        psum = ctx.enter_context(tc.psum_pool(name="psum", bufs=1))
+
+        offs_t = keep.tile([P, S // 16], U16, name="offs_t")
+        n1_t = keep.tile([P, S // 16], U16, name="n1_t")
+        n2_t = keep.tile([P, S // 16], U16, name="n2_t")
+        word_table = keep.tile([P, T], U32, name="word_table")
+        byte_table = keep.tile([P, T], U8, name="byte_table")
+        x_plane = keep.tile([P, S], U8, name="x_plane", align_bytes=64)
+        gain = keep.tile([P, PACK], F32, name="gain")
+
+        nc.vector.memset(byte_table[:, : T // 2].bitcast(I32), 0)
+        nc.gpsimd.memset(byte_table[:, T // 2 :].bitcast(I32), 0)
+        nc.vector.memset(x_plane[:].bitcast(I32), 0)
+
+        nc.sync.dma_start(offs_t[:], offs)
+        w1_rows = w1.rearrange("(p j) c -> p j c", j=PACK)
+        w2_rows = w2.rearrange("(p j) c -> p j c", j=PACK)
+        w1_raw = []
+        for h in range(2):
+            raw = keep.tile([P, PACK, HALF], F32, name=f"w1_raw{h}", tag=f"raw{h}")
+            nc.sync.dma_start(raw[:], w1_rows[:, :, h * HALF : (h + 1) * HALF])
+            w1_raw.append(raw)
+            if h == 0:
+                nc.sync.dma_start(byte_table[0:P:8, :].bitcast(I32), x_scales[0].bitcast(I32))
+        nc.sync.dma_start(n1_t[:], n1)
+        nc.sync.dma_start(n2_t[:], n2)
+        nc.sync.dma_start(word_table[:].bitcast(I32), x_words[0].rearrange("p n t -> p (n t)").bitcast(I32))
+        nc.sync.dma_start(gain[:], gn.rearrange("(p t) o -> p (t o)", t=PACK))
+
+        x_bytes = keep.tile([P, S], U8, name="x_bytes", tag="after_moves")
+        nc.vector.tensor_copy(x_bytes[:], byte_table[:].indirect(offs_t[:]))
+        for r in range(4):
+            nc.scalar.dma_start(x_plane[r:P:32, :].bitcast(I32), x_bytes[8 * r : P : 32, :].bitcast(I32))
+
+        w1_bf = keep.tile([P, PACK, P, PACK], BF16, name="w1_bf", align_bytes=64)
+        for h in range(2):
+            dst = w1_bf[:, :, h * 64 : (h + 1) * 64, :].rearrange("p t m j -> p m t j")
+            src = w1_raw[h][:].rearrange("p j (m t) -> p m t j", t=PACK)
+            if h == 0:
+                nc.scalar.activation(dst, src, ACT.Copy)
+            else:
+                nc.vector.tensor_copy(dst, src)
+        w1_codes = keep.tile([P, H], U32, name="w1_codes", align_bytes=64)
+        w1_plane = keep.tile([P, H], U8, name="w1_plane", align_bytes=64)
+        nc.vector.quantize_mx(w1_codes[:].bitcast(FP8X4), w1_plane[:], w1_bf[:].rearrange("p t m j -> p (t m j)"))
+
+        w2_raw = []
+        for h in range(2):
+            if h == 0:
+                w2_both = keep.tile([P, 2, PACK, HALF], F32, name="w2_both", tag="after_moves")
+            nc.sync.dma_start(w2_both[:, h], w2_rows[:, :, h * HALF : (h + 1) * HALF])
+            w2_raw.append(w2_both[:, h])
+
+        x_codes = keep.tile([P, S], U32, name="x_codes", align_bytes=64)
+        for h in range(2):
+            nc.vector.tensor_copy(x_codes[:, h * HALF : (h + 1) * HALF], word_table[:].indirect(offs_t[:, h * 16 : (h + 1) * 16]))
+
+        y_window = [keep.tile([P, S], F32, name=f"y_window{t}") for t in range(PACK)]
+        y_plain = [keep.tile([P, S], F32, name=f"y_plain{t}") for t in range(PACK)]
+
+        def first_product(t, cols, tag):
+            acc = psum.tile([P, cols.stop - cols.start], F32, name=f"y_acc{t}_{cols.start}", tag=tag)
+            wcols = slice(t * P, (t + 1) * P)
+            nc.tensor.matmul_mx(acc[:], w1_codes[:, wcols].bitcast(FP8X4), w1_plane[:, wcols], x_codes[:, cols].bitcast(FP8X4), x_plane[:, cols], start=True, stop=True)
+            return acc
+
+        low, high = slice(0, HALF), slice(HALF, S)
+        acc_low = first_product(0, low, "bank0")
+        nc.scalar.copy(y_window[0][:, low], acc_low[:])
+        nc.scalar.copy(y_plain[0][:, low], acc_low[:])
+        acc_high = first_product(0, high, "bank1")
+        nc.scalar.copy(y_window[0][:, high], acc_high[:])
+        for t in range(1, PACK):
+            acc = first_product(t, slice(0, S), f"bank{t + 1}")
+            nc.scalar.copy(y_window[t][:], acc[:])
+            if t == 1:
+                nc.scalar.copy(y_plain[t][:, low], acc[:, low])
+                nc.sync.dma_start(y_plain[0][:, high], y_window[0][:, high])
+                nc.sync.dma_start(y_plain[1][:, high], y_window[1][:, high])
+            else:
+                nc.sync.dma_start(y_plain[t][:], y_window[t][:])
+
+        w2_codes = keep.tile([P, N], U32, name="w2_codes", align_bytes=64)
+        w2_plane = keep.tile([P, N], U8, name="w2_plane", align_bytes=64)
+
+        def prepare_w2(h):
+            w2_bf = keep.tile([P, HALF, PACK], BF16, name=f"w2_bf{h}", align_bytes=64)
+            dst = w2_bf[:].rearrange("p (c i) j -> p c j i", i=4)
+            src = w2_raw[h].rearrange("p j (c i) -> p c j i", i=4)
+            if h == 0:
+                nc.vector.tensor_copy(dst, src)
+            else:
+                nc.scalar.copy(dst, src)
+            cols = slice(h * HALF, (h + 1) * HALF)
+            nc.vector.quantize_mx(w2_codes[:, cols].bitcast(FP8X4), w2_plane[:, cols], w2_bf[:].rearrange("p c j -> p (c j)"))
+
+        prepare_w2(0)
+        prepare_w2(1)
+
+        out_rows = out.rearrange("(b p) j -> p b j", p=P)
+        starts = [sum(CHUNKS[:ci]) for ci in range(len(CHUNKS))]
+        z_rows = [keep.tile([P, PACK, width], BF16, name=f"z_rows{ci}") for ci, width in enumerate(CHUNKS)]
+
+        def look_up(ci, t):
+            width = CHUNKS[ci]
+            cols = slice(starts[ci], starts[ci] + width)
+            lcols = slice(cols.start // 16, cols.stop // 16)
+            gate = ring.tile([P, width], F32, name=f"gate{ci}_{t}", tag="gate")
+            pos = ring.tile([P, width], F32, name=f"pos{ci}_{t}", tag="pos")
+            nc.vector.tensor_tensor(gate[:], y_window[t][:].indirect(n2_t[:, lcols]), y_plain[t][:, cols], ALU.add)
+            nc.vector.tensor_tensor(pos[:], y_window[t][:].indirect(n1_t[:, lcols]), y_plain[t][:, cols], ALU.subtract)
+            nc.scalar.activation(gate[:], gate[:], ACT.Sigmoid)
+            nc.scalar.activation(pos[:], pos[:], ACT.Relu, scale=-1.0)
+            nc.vector.scalar_tensor_tensor(z_rows[ci][:, t, :], pos[:], gain[:, t : t + 1], gate[:], ALU.mult, ALU.mult)
+
+        def second_product(ci):
+            width = CHUNKS[ci]
+            last = ci == len(CHUNKS) - 1
+            cols = slice(starts[ci], starts[ci] + width)
+            z_bf = keep.tile([P, width, PACK], BF16, name=f"z_bf{ci}", align_bytes=64)
+            dst = z_bf[:].rearrange("p (c i) t -> p c t i", i=4)
+            src = z_rows[ci][:].rearrange("p t (c i) -> p c t i", i=4)
+            if last:
+                nc.vector.tensor_copy(dst, src)
+            else:
+                nc.scalar.copy(dst, src)
+            z_codes = keep.tile([P, width], U32, name=f"z_codes{ci}", align_bytes=64)
+            z_plane = keep.tile([P, width], U8, name=f"z_plane{ci}", align_bytes=64)
+            nc.vector.quantize_mx(z_codes[:].bitcast(FP8X4), z_plane[:], z_bf[:].rearrange("p c t -> p (c t)"))
+            for pair in range(2):
+                acc = psum.tile([P, 2, width], F32, name=f"o_acc{ci}_{pair}", tag=f"bank{(5 + 2 * ci + pair) % 8}")
+                for e in range(2):
+                    mcols = slice((2 * pair + e) * P, (2 * pair + e + 1) * P)
+                    nc.tensor.matmul_mx(acc[:, e, :], w2_codes[:, mcols].bitcast(FP8X4), w2_plane[:, mcols], z_codes[:].bitcast(FP8X4), z_plane[:], start=True, stop=True)
+                staged = keep.tile([P, 2, width], F32, name=f"staged{ci}_{pair}")
+                if last and pair == 1:
+                    nc.vector.tensor_copy(staged[:], acc[:])
+                else:
+                    nc.scalar.copy(staged[:], acc[:])
+                nc.sync.dma_start(out_rows[:, 2 * pair : 2 * pair + 2, cols], staged[:])
+
+        for ci in range(len(CHUNKS)):
+            for t in range(PACK):
+                look_up(ci, t)
+            second_product(ci)

@@ -40,6 +40,10 @@ def tile_picked_hashgate_none_p_kernel(tc, x_words, x_scales, w1, gn, w2, offs, 
         nc.gpsimd.memset(byte_table[:, T // 2 :].bitcast(I32), 0)
         nc.vector.memset(x_plane[:].bitcast(I32), 0)
 
+        warm = keep.tile([P, 1], F32, name="warm")
+        nc.gpsimd.memset(warm[:], 0.0)
+        nc.scalar.activation(warm[:], warm[:], ACT.Sigmoid)
+
         nc.sync.dma_start(offs_t[:], offs)
         w1_rows = w1.rearrange("(p j) c -> p j c", j=PACK)
         w2_rows = w2.rearrange("(p j) c -> p j c", j=PACK)
@@ -55,7 +59,7 @@ def tile_picked_hashgate_none_p_kernel(tc, x_words, x_scales, w1, gn, w2, offs, 
         nc.sync.dma_start(word_table[:].bitcast(I32), x_words[0].rearrange("p n t -> p (n t)").bitcast(I32))
         nc.sync.dma_start(gain[:], gn.rearrange("(p t) o -> p (t o)", t=PACK))
 
-        x_bytes = keep.tile([P, S], U8, name="x_bytes", tag="after_moves")
+        x_bytes = keep.tile([P, S], U8, name="x_bytes")
         nc.vector.tensor_copy(x_bytes[:], byte_table[:].indirect(offs_t[:]))
         for r in range(4):
             nc.scalar.dma_start(x_plane[r:P:32, :].bitcast(I32), x_bytes[8 * r : P : 32, :].bitcast(I32))
@@ -65,17 +69,17 @@ def tile_picked_hashgate_none_p_kernel(tc, x_words, x_scales, w1, gn, w2, offs, 
             dst = w1_bf[:, :, h * 64 : (h + 1) * 64, :].rearrange("p t m j -> p m t j")
             src = w1_raw[h][:].rearrange("p j (m t) -> p m t j", t=PACK)
             if h == 0:
-                nc.scalar.activation(dst, src, ACT.Copy)
+                nc.scalar.copy(dst, src)
             else:
                 nc.vector.tensor_copy(dst, src)
-        w1_codes = keep.tile([P, H], U32, name="w1_codes", align_bytes=64)
+        w1_codes = keep.tile([P, H], U32, name="w1_codes", tag="w1_codes", align_bytes=64)
         w1_plane = keep.tile([P, H], U8, name="w1_plane", align_bytes=64)
         nc.vector.quantize_mx(w1_codes[:].bitcast(FP8X4), w1_plane[:], w1_bf[:].rearrange("p t m j -> p (t m j)"))
 
         w2_raw = []
         for h in range(2):
             if h == 0:
-                w2_both = keep.tile([P, 2, PACK, HALF], F32, name="w2_both", tag="after_moves")
+                w2_both = keep.tile([P, 2, PACK, HALF], F32, name="w2_both", tag="raw1")
             nc.sync.dma_start(w2_both[:, h], w2_rows[:, :, h * HALF : (h + 1) * HALF])
             w2_raw.append(w2_both[:, h])
 
@@ -98,56 +102,42 @@ def tile_picked_hashgate_none_p_kernel(tc, x_words, x_scales, w1, gn, w2, offs, 
         nc.scalar.copy(y_plain[0][:, low], acc_low[:])
         acc_high = first_product(0, high, "bank1")
         nc.scalar.copy(y_window[0][:, high], acc_high[:])
+        nc.sync.dma_start(y_plain[0][:, high], y_window[0][:, high])
         for t in range(1, PACK):
             acc = first_product(t, slice(0, S), f"bank{t + 1}")
             nc.scalar.copy(y_window[t][:], acc[:])
-            if t == 1:
-                nc.scalar.copy(y_plain[t][:, low], acc[:, low])
-                nc.sync.dma_start(y_plain[0][:, high], y_window[0][:, high])
-                nc.sync.dma_start(y_plain[1][:, high], y_window[1][:, high])
-            else:
-                nc.sync.dma_start(y_plain[t][:], y_window[t][:])
+            nc.scalar.copy(y_plain[t][:, low], acc[:, low])
+            nc.sync.dma_start(y_plain[t][:, high], y_window[t][:, high])
 
         w2_codes = keep.tile([P, N], U32, name="w2_codes", align_bytes=64)
         w2_plane = keep.tile([P, N], U8, name="w2_plane", align_bytes=64)
+        w2_bf = keep.tile([P, N, PACK], BF16, name="w2_bf", tag="w1_codes", align_bytes=64)
 
-        def prepare_w2(h):
-            w2_bf = keep.tile([P, HALF, PACK], BF16, name=f"w2_bf{h}", align_bytes=64)
-            dst = w2_bf[:].rearrange("p (c i) j -> p c j i", i=4)
-            src = w2_raw[h].rearrange("p j (c i) -> p c j i", i=4)
-            if h == 0:
-                nc.vector.tensor_copy(dst, src)
-            else:
-                nc.scalar.copy(dst, src)
-            cols = slice(h * HALF, (h + 1) * HALF)
-            nc.vector.quantize_mx(w2_codes[:, cols].bitcast(FP8X4), w2_plane[:, cols], w2_bf[:].rearrange("p c j -> p (c j)"))
-
-        prepare_w2(0)
-        prepare_w2(1)
+        def round_w2(b):
+            dst = w2_bf[:, b * P : (b + 1) * P, :].rearrange("p (c i) j -> p c j i", i=4)
+            src = w2_raw[b // 2][:, :, (b % 2) * P : (b % 2 + 1) * P].rearrange("p j (c i) -> p c j i", i=4)
+            nc.scalar.copy(dst, src)
 
         out_rows = out.rearrange("(b p) j -> p b j", p=P)
-        starts = [sum(CHUNKS[:ci]) for ci in range(len(CHUNKS))]
-        z_rows = [keep.tile([P, PACK, width], BF16, name=f"z_rows{ci}") for ci, width in enumerate(CHUNKS)]
+        z_rows = keep.tile([P, PACK, S], BF16, name="z_rows")
 
-        def look_up(ci, t):
-            width = CHUNKS[ci]
-            cols = slice(starts[ci], starts[ci] + width)
+        def look_up(t, cols):
+            width = cols.stop - cols.start
             lcols = slice(cols.start // 16, cols.stop // 16)
-            gate = ring.tile([P, width], F32, name=f"gate{ci}_{t}", tag="gate")
-            pos = ring.tile([P, width], F32, name=f"pos{ci}_{t}", tag="pos")
+            gate = ring.tile([P, width], F32, name=f"gate{cols.start}_{t}", tag="gate")
+            pos = ring.tile([P, width], F32, name=f"pos{cols.start}_{t}", tag="pos")
             nc.vector.tensor_tensor(gate[:], y_window[t][:].indirect(n2_t[:, lcols]), y_plain[t][:, cols], ALU.add)
             nc.vector.tensor_tensor(pos[:], y_window[t][:].indirect(n1_t[:, lcols]), y_plain[t][:, cols], ALU.subtract)
             nc.scalar.activation(gate[:], gate[:], ACT.Sigmoid)
             nc.scalar.activation(pos[:], pos[:], ACT.Relu, scale=-1.0)
-            nc.vector.scalar_tensor_tensor(z_rows[ci][:, t, :], pos[:], gain[:, t : t + 1], gate[:], ALU.mult, ALU.mult)
+            nc.vector.scalar_tensor_tensor(z_rows[:, t, cols], pos[:], gain[:, t : t + 1], gate[:], ALU.mult, ALU.mult)
 
-        def second_product(ci):
-            width = CHUNKS[ci]
-            last = ci == len(CHUNKS) - 1
-            cols = slice(starts[ci], starts[ci] + width)
+        def second_product(ci, cols):
+            width = cols.stop - cols.start
+            last = cols.stop == S
             z_bf = keep.tile([P, width, PACK], BF16, name=f"z_bf{ci}", align_bytes=64)
             dst = z_bf[:].rearrange("p (c i) t -> p c t i", i=4)
-            src = z_rows[ci][:].rearrange("p t (c i) -> p c t i", i=4)
+            src = z_rows[:, :, cols].rearrange("p t (c i) -> p c t i", i=4)
             if last:
                 nc.vector.tensor_copy(dst, src)
             else:
@@ -167,7 +157,17 @@ def tile_picked_hashgate_none_p_kernel(tc, x_words, x_scales, w1, gn, w2, offs, 
                     nc.scalar.copy(staged[:], acc[:])
                 nc.sync.dma_start(out_rows[:, 2 * pair : 2 * pair + 2, cols], staged[:])
 
-        for ci in range(len(CHUNKS)):
-            for t in range(PACK):
-                look_up(ci, t)
-            second_product(ci)
+        third, fourth = slice(HALF, HALF + P), slice(HALF + P, S)
+        for t in range(PACK):
+            look_up(t, low)
+            round_w2(t)
+        nc.vector.quantize_mx(w2_codes[:].bitcast(FP8X4), w2_plane[:], w2_bf[:].rearrange("p c j -> p (c j)"))
+        second_product(0, low)
+        look_up(0, high)
+        look_up(1, high)
+        look_up(2, third)
+        look_up(3, third)
+        second_product(1, third)
+        look_up(2, fourth)
+        look_up(3, fourth)
+        second_product(2, fourth)

@@ -54,8 +54,8 @@ def tile_picked_hashgate_none_p_kernel(tc, x_words, x_scales, w1, gn, w2, offs, 
             w1_raw.append(raw)
             if h == 0:
                 nc.sync.dma_start(byte_table[0:P:8, :].bitcast(I32), x_scales[0].bitcast(I32))
-        nc.sync.dma_start(n1_t[:], n1)
-        nc.sync.dma_start(n2_t[:], n2)
+                nc.sync.dma_start(n1_t[:], n1)
+                nc.sync.dma_start(n2_t[:], n2)
         nc.sync.dma_start(word_table[:].bitcast(I32), x_words[0].rearrange("p n t -> p (n t)").bitcast(I32))
         nc.sync.dma_start(gain[:], gn.rearrange("(p t) o -> p (t o)", t=PACK))
 
@@ -87,8 +87,9 @@ def tile_picked_hashgate_none_p_kernel(tc, x_words, x_scales, w1, gn, w2, offs, 
         for h in range(2):
             nc.vector.tensor_copy(x_codes[:, h * HALF : (h + 1) * HALF], word_table[:].indirect(offs_t[:, h * 16 : (h + 1) * 16]))
 
-        y_window = [keep.tile([P, S], F32, name=f"y_window{t}") for t in range(PACK)]
-        y_plain = [keep.tile([P, S], F32, name=f"y_plain{t}") for t in range(PACK)]
+        wide = keep.tile([P, 2 * S], F32, name="wide")
+        y_window = [wide if t == 1 else keep.tile([P, S], F32, name=f"y_window{t}") for t in range(PACK)]
+        y_plain = [wide[:, S:] if t == 0 else keep.tile([P, S], F32, name=f"y_plain{t}")[:] for t in range(PACK)]
 
         def first_product(t, cols, tag):
             acc = psum.tile([P, cols.stop - cols.start], F32, name=f"y_acc{t}_{cols.start}", tag=tag)
@@ -102,12 +103,14 @@ def tile_picked_hashgate_none_p_kernel(tc, x_words, x_scales, w1, gn, w2, offs, 
         nc.scalar.copy(y_plain[0][:, low], acc_low[:])
         acc_high = first_product(0, high, "bank1")
         nc.scalar.copy(y_window[0][:, high], acc_high[:])
-        nc.sync.dma_start(y_plain[0][:, high], y_window[0][:, high])
+        nc.scalar.copy(y_plain[0][:, high], acc_high[:])
         for t in range(1, PACK):
             acc = first_product(t, slice(0, S), f"bank{t + 1}")
-            nc.scalar.copy(y_window[t][:], acc[:])
-            nc.scalar.copy(y_plain[t][:, low], acc[:, low])
-            nc.sync.dma_start(y_plain[t][:, high], y_window[t][:, high])
+            nc.scalar.copy(y_window[t][:, :S], acc[:])
+            if t == 1:
+                nc.scalar.copy(y_plain[t], acc[:])
+            else:
+                nc.sync.dma_start(y_plain[t], y_window[t][:])
 
         w2_codes = keep.tile([P, N], U32, name="w2_codes", align_bytes=64)
         w2_plane = keep.tile([P, N], U8, name="w2_plane", align_bytes=64)
@@ -158,16 +161,14 @@ def tile_picked_hashgate_none_p_kernel(tc, x_words, x_scales, w1, gn, w2, offs, 
                 nc.sync.dma_start(out_rows[:, 2 * pair : 2 * pair + 2, cols], staged[:])
 
         third, fourth = slice(HALF, HALF + P), slice(HALF + P, S)
-        for t in range(PACK):
-            look_up(t, low)
-            round_w2(t)
+        for b, (t, cols) in enumerate(((0, low), (0, high), (1, slice(0, S)), (2, low))):
+            look_up(t, cols)
+            round_w2(b)
         nc.vector.quantize_mx(w2_codes[:].bitcast(FP8X4), w2_plane[:], w2_bf[:].rearrange("p c j -> p (c j)"))
+        look_up(3, low)
         second_product(0, low)
-        look_up(0, high)
-        look_up(1, high)
-        look_up(2, third)
+        look_up(2, high)
         look_up(3, third)
         second_product(1, third)
-        look_up(2, fourth)
         look_up(3, fourth)
         second_product(2, fourth)

from contextlib import ExitStack

import concourse.mybir as mybir

K, T, S, H, N = 512, 2048, 512, 512, 512
FLOPS = 2 * K * H * S + 2 * H * N * S

F32 = mybir.dt.float32
BF16 = mybir.dt.bfloat16
I32 = mybir.dt.int32
U32 = mybir.dt.uint32
U16 = mybir.dt.uint16
U8 = mybir.dt.uint8
FP8X4 = mybir.dt.float8_e4m3fn_x4
ALU = mybir.AluOpType
ACT = mybir.ActivationFunctionType

P = 128
PACK = 4
HALF = 256
CHUNKS = (256, 128, 128)


def tile_picked_hashgate_none_p_kernel(tc, x_words, x_scales, w1, gn, w2, offs, n1, n2, out):
    nc = tc.nc
    with ExitStack() as ctx:
        keep = ctx.enter_context(tc.tile_pool(name="keep", bufs=1))
        ring = ctx.enter_context(tc.tile_pool(name="ring", bufs=3))
        psum = ctx.enter_context(tc.psum_pool(name="psum", bufs=1))

        offs_t = keep.tile([P, S // 16], U16, name="offs_t")
        n1_t = keep.tile([P, S // 16], U16, name="n1_t")
        n2_t = keep.tile([P, S // 16], U16, name="n2_t")
        word_table = keep.tile([P, T], U32, name="word_table")
        byte_table = keep.tile([P, T], U8, name="byte_table")
        x_plane = keep.tile([P, S], U8, name="x_plane", align_bytes=64)
        gain = keep.tile([P, PACK], F32, name="gain")

        nc.vector.memset(byte_table[:, : T // 2].bitcast(I32), 0)
        nc.gpsimd.memset(byte_table[:, T // 2 :].bitcast(I32), 0)
        nc.vector.memset(x_plane[:].bitcast(I32), 0)

        warm = keep.tile([P, 1], F32, name="warm")
        nc.gpsimd.memset(warm[:], 0.0)
        nc.scalar.activation(warm[:], warm[:], ACT.Sigmoid)

        nc.sync.dma_start(offs_t[:], offs)
        w1_rows = w1.rearrange("(p j) c -> p j c", j=PACK)
        w2_rows = w2.rearrange("(p j) c -> p j c", j=PACK)
        w1_raw = []
        for h in range(2):
            raw = keep.tile([P, PACK, HALF], F32, name=f"w1_raw{h}", tag=f"raw{h}")
            nc.sync.dma_start(raw[:], w1_rows[:, :, h * HALF : (h + 1) * HALF])
            w1_raw.append(raw)
            if h == 0:
                nc.sync.dma_start(byte_table[0:P:8, :].bitcast(I32), x_scales[0].bitcast(I32))
                nc.sync.dma_start(n1_t[:], n1)
                nc.sync.dma_start(n2_t[:], n2)
        nc.sync.dma_start(word_table[:].bitcast(I32), x_words[0].rearrange("p n t -> p (n t)").bitcast(I32))
        nc.sync.dma_start(gain[:], gn.rearrange("(p t) o -> p (t o)", t=PACK))

        x_bytes = keep.tile([P, S], U8, name="x_bytes")
        nc.vector.tensor_copy(x_bytes[:], byte_table[:].indirect(offs_t[:]))
        for r in range(4):
            nc.scalar.dma_start(x_plane[r:P:32, :].bitcast(I32), x_bytes[8 * r : P : 32, :].bitcast(I32))

        w1_bf = keep.tile([P, PACK, P, PACK], BF16, name="w1_bf", align_bytes=64)
        for h in range(2):
            dst = w1_bf[:, :, h * 64 : (h + 1) * 64, :].rearrange("p t m j -> p m t j")
            src = w1_raw[h][:].rearrange("p j (m t) -> p m t j", t=PACK)
            if h == 0:
                nc.scalar.copy(dst, src)
            else:
                nc.vector.tensor_copy(dst, src)
        w1_codes = keep.tile([P, H], U32, name="w1_codes", tag="w1_codes", align_bytes=64)
        w1_plane = keep.tile([P, H], U8, name="w1_plane", align_bytes=64)
        nc.vector.quantize_mx(w1_codes[:].bitcast(FP8X4), w1_plane[:], w1_bf[:].rearrange("p t m j -> p (t m j)"))

        w2_raw = []
        for h in range(2):
            if h == 0:
                w2_both = keep.tile([P, 2, PACK, HALF], F32, name="w2_both", tag="raw1")
            nc.sync.dma_start(w2_both[:, h], w2_rows[:, :, h * HALF : (h + 1) * HALF])
            w2_raw.append(w2_both[:, h])

        x_codes = keep.tile([P, S], U32, name="x_codes", align_bytes=64)
        for h in range(2):
            nc.vector.tensor_copy(x_codes[:, h * HALF : (h + 1) * HALF], word_table[:].indirect(offs_t[:, h * 16 : (h + 1) * 16]))

        wide = keep.tile([P, 2 * S], F32, name="wide")
        y_window = [wide if t == 1 else keep.tile([P, S], F32, name=f"y_window{t}") for t in range(PACK)]
        y_plain = [wide[:, S:] if t == 0 else keep.tile([P, S], F32, name=f"y_plain{t}")[:] for t in range(PACK)]

        def first_product(t, cols, tag):
            acc = psum.tile([P, cols.stop - cols.start], F32, name=f"y_acc{t}_{cols.start}", tag=tag)
            wcols = slice(t * P, (t + 1) * P)
            nc.tensor.matmul_mx(acc[:], w1_codes[:, wcols].bitcast(FP8X4), w1_plane[:, wcols], x_codes[:, cols].bitcast(FP8X4), x_plane[:, cols], start=True, stop=True)
            return acc

        low, high = slice(0, HALF), slice(HALF, S)
        acc_low = first_product(0, low, "bank0")
        nc.scalar.copy(y_window[0][:, low], acc_low[:])
        nc.scalar.copy(y_plain[0][:, low], acc_low[:])
        acc_high = first_product(0, high, "bank1")
        nc.scalar.copy(y_window[0][:, high], acc_high[:])
        nc.scalar.copy(y_plain[0][:, high], acc_high[:])
        for t in range(1, PACK):
            acc = first_product(t, slice(0, S), f"bank{t + 1}")
            nc.scalar.copy(y_window[t][:, :S], acc[:])
            if t == 1:
                nc.scalar.copy(y_plain[t], acc[:])
            else:
                nc.sync.dma_start(y_plain[t], y_window[t][:])

        w2_codes = keep.tile([P, N], U32, name="w2_codes", align_bytes=64)
        w2_plane = keep.tile([P, N], U8, name="w2_plane", align_bytes=64)
        w2_bf = keep.tile([P, N, PACK], BF16, name="w2_bf", tag="w1_codes", align_bytes=64)

        def round_w2(b):
            dst = w2_bf[:, b * P : (b + 1) * P, :].rearrange("p (c i) j -> p c j i", i=4)
            src = w2_raw[b // 2][:, :, (b % 2) * P : (b % 2 + 1) * P].rearrange("p j (c i) -> p c j i", i=4)
            nc.scalar.copy(dst, src)

        out_rows = out.rearrange("(b p) j -> p b j", p=P)
        z_rows = keep.tile([P, PACK, S], BF16, name="z_rows")

        def look_up(t, cols):
            width = cols.stop - cols.start
            lcols = slice(cols.start // 16, cols.stop // 16)
            gate = ring.tile([P, width], F32, name=f"gate{cols.start}_{t}", tag="gate")
            pos = ring.tile([P, width], F32, name=f"pos{cols.start}_{t}", tag="pos")
            nc.vector.tensor_tensor(gate[:], y_window[t][:].indirect(n2_t[:, lcols]), y_plain[t][:, cols], ALU.add)
            nc.vector.tensor_tensor(pos[:], y_window[t][:].indirect(n1_t[:, lcols]), y_plain[t][:, cols], ALU.subtract)
            nc.scalar.activation(gate[:], gate[:], ACT.Sigmoid)
            nc.scalar.activation(pos[:], pos[:], ACT.Relu, scale=-1.0)
            nc.vector.scalar_tensor_tensor(z_rows[:, t, cols], pos[:], gain[:, t : t + 1], gate[:], ALU.mult, ALU.mult)

        def second_product(ci, cols):
            width = cols.stop - cols.start
            last = cols.stop == S
            z_bf = keep.tile([P, width, PACK], BF16, name=f"z_bf{ci}", align_bytes=64)
            dst = z_bf[:].rearrange("p (c i) t -> p c t i", i=4)
            src = z_rows[:, :, cols].rearrange("p t (c i) -> p c t i", i=4)
            if last:
                nc.vector.tensor_copy(dst, src)
            else:
                nc.scalar.copy(dst, src)
            z_codes = keep.tile([P, width], U32, name=f"z_codes{ci}", align_bytes=64)
            z_plane = keep.tile([P, width], U8, name=f"z_plane{ci}", align_bytes=64)
            nc.vector.quantize_mx(z_codes[:].bitcast(FP8X4), z_plane[:], z_bf[:].rearrange("p c t -> p (c t)"))
            for pair in range(2):
                acc = psum.tile([P, 2, width], F32, name=f"o_acc{ci}_{pair}", tag=f"bank{(5 + 2 * ci + pair) % 8}")
                for e in range(2):
                    mcols = slice((2 * pair + e) * P, (2 * pair + e + 1) * P)
                    nc.tensor.matmul_mx(acc[:, e, :], w2_codes[:, mcols].bitcast(FP8X4), w2_plane[:, mcols], z_codes[:].bitcast(FP8X4), z_plane[:], start=True, stop=True)
                staged = keep.tile([P, 2, width], F32, name=f"staged{ci}_{pair}")
                if last and pair == 1:
                    nc.vector.tensor_copy(staged[:], acc[:])
                else:
                    nc.scalar.copy(staged[:], acc[:])
                nc.sync.dma_start(out_rows[:, 2 * pair : 2 * pair + 2, cols], staged[:])

        third, fourth = slice(HALF, HALF + P), slice(HALF + P, S)
        for b, (t, cols) in enumerate(((0, low), (0, high), (1, slice(0, S)), (2, low))):
            look_up(t, cols)
            round_w2(b)
        nc.vector.quantize_mx(w2_codes[:].bitcast(FP8X4), w2_plane[:], w2_bf[:].rearrange("p c j -> p (c j)"))
        look_up(3, low)
        second_product(0, low)
        look_up(2, high)
        look_up(3, third)
        second_product(1, third)
        look_up(3, fourth)
        second_product(2, fourth)
